import numpy as np
import ml_dtypes

BF16 = ml_dtypes.bfloat16


def bf(x):
    return np.asarray(x, np.float32).astype(BF16)


def f32(x):
    return np.asarray(x, np.float32)


def f64(x):
    return np.asarray(x).astype(np.float64)


def striped(idx):
    return np.tile(idx.reshape(-1, 16).T, (8, 1))


S, K, H, M, N, E, Q = 512, 512, 256, 512, 256, 2, 128


def sigmoid(v):
    return 1.0 / (1.0 + np.exp(-v))


def setup_inputs():
    return {"base": bf(np.random.standard_normal((M, S))), "x": bf(np.random.standard_normal((K, N))), "w": bf(np.random.standard_normal((E, K, H)) / np.sqrt(K)), "b": f32(0.5 * np.random.standard_normal((H, E))), "w2": bf(1.5 * np.random.standard_normal((E, H, M)) / np.sqrt(H)), "offs": striped(np.random.permutation(S)[:N])}


def reference(base, x, w, b, w2, offs):
    idx = offs[:16].T.reshape(-1)
    z = f64(base).copy()
    for e in range(E):
        t = f64(w)[e].T @ f64(x)[:, e * Q : (e + 1) * Q] + f64(b)[:, e : e + 1]
        t = t * sigmoid(t)
        z[:, idx[e * Q : (e + 1) * Q]] += f64(w2)[e].T @ t
    return z

@@ -1,0 +1,86 @@
+import concourse.mybir as mybir
+from concourse.masks import make_identity
+
+BF16, F32, U16 = mybir.dt.bfloat16, mybir.dt.float32, mybir.dt.uint16
+SILU = mybir.ActivationFunctionType.Silu
+
+P = 128
+S = 512
+K, H, M = 512, 256, 512
+E, Q = 2, 128
+N = E * Q
+
+FLOPS = 2 * N * K * H + 2 * N * H * M
+
+
+def tile_rows_ffnback_silu_kernel(tc, base, x, w, b, w2, offs, out):
+    nc = tc.nc
+    k_blocks, h_blocks, m_blocks = K // P, H // P, M // P
+    with (
+        tc.tile_pool(name="held", bufs=1) as held,
+        tc.psum_pool(name="psum", bufs=1) as psum,
+    ):
+        x_tile = held.tile([P, k_blocks, N], BF16)
+        nc.sync.dma_start(x_tile[:], x.rearrange("(p a) n -> p a n", p=P))
+        w_tiles = []
+        for e in range(E):
+            w_tile = held.tile([P, k_blocks, H], BF16, name=f"w_{e}")
+            nc.sync.dma_start(w_tile[:], w[e].rearrange("(p a) h -> p a h", p=P))
+            w_tiles.append(w_tile)
+        base_tile = held.tile([P, m_blocks, S], BF16)
+        nc.sync.dma_start(base_tile[:], base.rearrange("(a p) s -> p a s", p=P))
+        offsets = held.tile([P, N // 16], U16)
+        nc.sync.dma_start(offsets[:], offs)
+        w2_tiles = []
+        for e in range(E):
+            w2_tile = held.tile([P, h_blocks, M], BF16, name=f"w2_{e}")
+            nc.sync.dma_start(w2_tile[:], w2[e].rearrange("(c p) m -> p c m", p=P))
+            w2_tiles.append(w2_tile)
+        bias = held.tile([P, h_blocks, E], F32)
+        nc.scalar.dma_start(bias[:], b.rearrange("(c p) e -> p c e", p=P))
+
+        ident = held.tile([P, P], BF16)
+        make_identity(nc, ident[:])
+
+        h_tiles = {}
+        for e in range(E):
+            for c in range(h_blocks):
+                pre = psum.tile([P, Q], F32, name=f"pre_{e}_{c}")
+                for a in range(k_blocks):
+                    nc.tensor.matmul(
+                        pre[:],
+                        w_tiles[e][:, a, c * P : (c + 1) * P],
+                        x_tile[:, a, e * Q : (e + 1) * Q],
+                        start=a == 0,
+                        stop=a == k_blocks - 1,
+                    )
+                h_tile = held.tile([P, Q], BF16, name=f"h_{e}_{c}")
+                nc.scalar.activation(h_tile[:], pre[:], SILU, bias=bias[:, c, e : e + 1])
+                h_tiles[e, c] = h_tile
+
+        windows = []
+        for a in range(m_blocks):
+            window = psum.tile([P, S], F32, name=f"window_{a}")
+            nc.tensor.matmul(window[:], ident[:], base_tile[:, a, :], start=True, stop=False)
+            windows.append(window)
+
+        for e in range(E):
+            places = offsets[:, e * (Q // 16) : (e + 1) * (Q // 16)]
+            for a in range(m_blocks):
+                for c in range(h_blocks):
+                    nc.tensor.matmul(
+                        windows[a][:].indirect(places),
+                        w2_tiles[e][:, c, a * P : (a + 1) * P],
+                        h_tiles[e, c][:],
+                        start=False,
+                        stop=e == E - 1 and c == h_blocks - 1,
+                    )
+
+        out_rows = out.rearrange("(a p) s -> a p s", p=P)
+        for a in range(m_blocks):
+            z = held.tile([P, S], F32, name=f"z_{a}")
+            if a % 2 == 0:
+                nc.vector.tensor_copy(z[:], windows[a][:])
+            else:
+                nc.scalar.copy(z[:], windows[a][:])
+            nc.sync.dma_start(out_rows[a], z[:])

@@ -9,6 +9,7 @@ S = 512
 K, H, M = 512, 256, 512
 E, Q = 2, 128
 N = E * Q
+WARM_UPS = 4
 
 FLOPS = 2 * N * K * H + 2 * N * H * M
 
@@ -20,27 +21,37 @@ def tile_rows_ffnback_silu_kernel(tc, base, x, w, b, w2, offs, out):
         tc.tile_pool(name="held", bufs=1) as held,
         tc.psum_pool(name="psum", bufs=1) as psum,
     ):
-        x_tile = held.tile([P, k_blocks, N], BF16)
-        nc.sync.dma_start(x_tile[:], x.rearrange("(p a) n -> p a n", p=P))
-        w_tiles = []
-        for e in range(E):
-            w_tile = held.tile([P, k_blocks, H], BF16, name=f"w_{e}")
-            nc.sync.dma_start(w_tile[:], w[e].rearrange("(p a) h -> p a h", p=P))
-            w_tiles.append(w_tile)
-        base_tile = held.tile([P, m_blocks, S], BF16)
-        nc.sync.dma_start(base_tile[:], base.rearrange("(a p) s -> p a s", p=P))
-        offsets = held.tile([P, N // 16], U16)
-        nc.sync.dma_start(offsets[:], offs)
-        w2_tiles = []
-        for e in range(E):
-            w2_tile = held.tile([P, h_blocks, M], BF16, name=f"w2_{e}")
-            nc.sync.dma_start(w2_tile[:], w2[e].rearrange("(c p) m -> p c m", p=P))
-            w2_tiles.append(w2_tile)
-        bias = held.tile([P, h_blocks, E], F32)
-        nc.scalar.dma_start(bias[:], b.rearrange("(c p) e -> p c e", p=P))
+        zeros = held.tile([P, S], BF16)
+        nc.vector.memset(zeros[:], 0.0)
+        idle_bank = psum.tile([P, S], F32, tag="pre_0_0")
+        for turn in range(WARM_UPS):
+            nc.tensor.matmul(idle_bank[:], zeros[:, :P], zeros[:], start=True, stop=True)
+        early = held.tile([P, 1], BF16)
+        nc.scalar.activation(early[:], zeros[:, :1], SILU)
 
         ident = held.tile([P, P], BF16)
         make_identity(nc, ident[:])
+
+        base_tile = held.tile([P, m_blocks, S], BF16)
+        nc.sync.dma_start(base_tile[:], base.rearrange("(a p) s -> p a s", p=P))
+        x_tile = held.tile([P, k_blocks, N], BF16)
+        nc.sync.dma_start(x_tile[:], x.rearrange("(p a) n -> p a n", p=P))
+        w_tiles = [held.tile([P, k_blocks, H], BF16, name=f"w_{e}") for e in range(E)]
+        w2_tiles = [held.tile([P, h_blocks, M], BF16, name=f"w2_{e}") for e in range(E)]
+        bias = held.tile([P, h_blocks, E], F32)
+        offsets = held.tile([P, N // 16], U16)
+        nc.sync.dma_start(w_tiles[0][:], w[0].rearrange("(p a) h -> p a h", p=P))
+        nc.sync.dma_start(bias[:], b.rearrange("(p c) e -> p c e", p=P))
+        nc.sync.dma_start(w_tiles[1][:], w[1].rearrange("(p a) h -> p a h", p=P))
+        nc.sync.dma_start(offsets[:], offs)
+        for e in range(E):
+            nc.sync.dma_start(w2_tiles[e][:], w2[e].rearrange("(p c) m -> p c m", p=P))
+
+        windows = []
+        for a in range(m_blocks):
+            window = psum.tile([P, S], F32, name=f"window_{a}")
+            nc.tensor.matmul(window[:], ident[:], base_tile[:, a, :], start=True, stop=False)
+            windows.append(window)
 
         h_tiles = {}
         for e in range(E):
@@ -49,7 +60,7 @@ def tile_rows_ffnback_silu_kernel(tc, base, x, w, b, w2, offs, out):
                 for a in range(k_blocks):
                     nc.tensor.matmul(
                         pre[:],
-                        w_tiles[e][:, a, c * P : (c + 1) * P],
+                        w_tiles[e][:, a, c::h_blocks],
                         x_tile[:, a, e * Q : (e + 1) * Q],
                         start=a == 0,
                         stop=a == k_blocks - 1,
@@ -57,12 +68,6 @@ def tile_rows_ffnback_silu_kernel(tc, base, x, w, b, w2, offs, out):
                 h_tile = held.tile([P, Q], BF16, name=f"h_{e}_{c}")
                 nc.scalar.activation(h_tile[:], pre[:], SILU, bias=bias[:, c, e : e + 1])
                 h_tiles[e, c] = h_tile
-
-        windows = []
-        for a in range(m_blocks):
-            window = psum.tile([P, S], F32, name=f"window_{a}")
-            nc.tensor.matmul(window[:], ident[:], base_tile[:, a, :], start=True, stop=False)
-            windows.append(window)
 
         for e in range(E):
             places = offsets[:, e * (Q // 16) : (e + 1) * (Q // 16)]

@@ -32,8 +32,6 @@ def tile_rows_ffnback_silu_kernel(tc, base, x, w, b, w2, offs, out):
         ident = held.tile([P, P], BF16)
         make_identity(nc, ident[:])
 
-        base_tile = held.tile([P, m_blocks, S], BF16)
-        nc.sync.dma_start(base_tile[:], base.rearrange("(a p) s -> p a s", p=P))
         x_tile = held.tile([P, k_blocks, N], BF16)
         nc.sync.dma_start(x_tile[:], x.rearrange("(p a) n -> p a n", p=P))
         w_tiles = [held.tile([P, k_blocks, H], BF16, name=f"w_{e}") for e in range(E)]
@@ -43,15 +41,15 @@ def tile_rows_ffnback_silu_kernel(tc, base, x, w, b, w2, offs, out):
         nc.sync.dma_start(w_tiles[0][:], w[0].rearrange("(p a) h -> p a h", p=P))
         nc.sync.dma_start(bias[:], b.rearrange("(p c) e -> p c e", p=P))
         nc.sync.dma_start(w_tiles[1][:], w[1].rearrange("(p a) h -> p a h", p=P))
+        base_rows = base.rearrange("(a p) s -> p a s", p=P)
+        base_tiles = []
+        for pair in range(0, m_blocks, 2):
+            base_tile = held.tile([P, 2, S], BF16, name=f"base_{pair}")
+            nc.sync.dma_start(base_tile[:], base_rows[:, pair : pair + 2, :])
+            base_tiles.append(base_tile)
         nc.sync.dma_start(offsets[:], offs)
         for e in range(E):
             nc.sync.dma_start(w2_tiles[e][:], w2[e].rearrange("(p c) m -> p c m", p=P))
-
-        windows = []
-        for a in range(m_blocks):
-            window = psum.tile([P, S], F32, name=f"window_{a}")
-            nc.tensor.matmul(window[:], ident[:], base_tile[:, a, :], start=True, stop=False)
-            windows.append(window)
 
         h_tiles = {}
         for e in range(E):
@@ -69,9 +67,15 @@ def tile_rows_ffnback_silu_kernel(tc, base, x, w, b, w2, offs, out):
                 nc.scalar.activation(h_tile[:], pre[:], SILU, bias=bias[:, c, e : e + 1])
                 h_tiles[e, c] = h_tile
 
-        for e in range(E):
-            places = offsets[:, e * (Q // 16) : (e + 1) * (Q // 16)]
-            for a in range(m_blocks):
+        windows = []
+        for a in range(m_blocks):
+            window = psum.tile([P, S], F32, name=f"window_{a}")
+            nc.tensor.matmul(window[:], ident[:], base_tiles[a // 2][:, a % 2, :], start=True, stop=False)
+            windows.append(window)
+
+        for a in range(m_blocks):
+            for e in range(E):
+                places = offsets[:, e * (Q // 16) : (e + 1) * (Q // 16)]
                 for c in range(h_blocks):
                     nc.tensor.matmul(
                         windows[a][:].indirect(places),

import concourse.mybir as mybir
from concourse.masks import make_identity

BF16, F32, U16 = mybir.dt.bfloat16, mybir.dt.float32, mybir.dt.uint16
SILU = mybir.ActivationFunctionType.Silu

P = 128
S = 512
K, H, M = 512, 256, 512
E, Q = 2, 128
N = E * Q
WARM_UPS = 4

FLOPS = 2 * N * K * H + 2 * N * H * M


def tile_rows_ffnback_silu_kernel(tc, base, x, w, b, w2, offs, out):
    nc = tc.nc
    k_blocks, h_blocks, m_blocks = K // P, H // P, M // P
    with (
        tc.tile_pool(name="held", bufs=1) as held,
        tc.psum_pool(name="psum", bufs=1) as psum,
    ):
        zeros = held.tile([P, S], BF16)
        nc.vector.memset(zeros[:], 0.0)
        idle_bank = psum.tile([P, S], F32, tag="pre_0_0")
        for turn in range(WARM_UPS):
            nc.tensor.matmul(idle_bank[:], zeros[:, :P], zeros[:], start=True, stop=True)
        early = held.tile([P, 1], BF16)
        nc.scalar.activation(early[:], zeros[:, :1], SILU)

        ident = held.tile([P, P], BF16)
        make_identity(nc, ident[:])

        x_tile = held.tile([P, k_blocks, N], BF16)
        nc.sync.dma_start(x_tile[:], x.rearrange("(p a) n -> p a n", p=P))
        w_tiles = [held.tile([P, k_blocks, H], BF16, name=f"w_{e}") for e in range(E)]
        w2_tiles = [held.tile([P, h_blocks, M], BF16, name=f"w2_{e}") for e in range(E)]
        bias = held.tile([P, h_blocks, E], F32)
        offsets = held.tile([P, N // 16], U16)
        nc.sync.dma_start(w_tiles[0][:], w[0].rearrange("(p a) h -> p a h", p=P))
        nc.sync.dma_start(bias[:], b.rearrange("(p c) e -> p c e", p=P))
        nc.sync.dma_start(w_tiles[1][:], w[1].rearrange("(p a) h -> p a h", p=P))
        base_rows = base.rearrange("(a p) s -> p a s", p=P)
        base_tiles = []
        for pair in range(0, m_blocks, 2):
            base_tile = held.tile([P, 2, S], BF16, name=f"base_{pair}")
            nc.sync.dma_start(base_tile[:], base_rows[:, pair : pair + 2, :])
            base_tiles.append(base_tile)
        nc.sync.dma_start(offsets[:], offs)
        for e in range(E):
            nc.sync.dma_start(w2_tiles[e][:], w2[e].rearrange("(p c) m -> p c m", p=P))

        h_tiles = {}
        for e in range(E):
            for c in range(h_blocks):
                pre = psum.tile([P, Q], F32, name=f"pre_{e}_{c}")
                for a in range(k_blocks):
                    nc.tensor.matmul(
                        pre[:],
                        w_tiles[e][:, a, c::h_blocks],
                        x_tile[:, a, e * Q : (e + 1) * Q],
                        start=a == 0,
                        stop=a == k_blocks - 1,
                    )
                h_tile = held.tile([P, Q], BF16, name=f"h_{e}_{c}")
                nc.scalar.activation(h_tile[:], pre[:], SILU, bias=bias[:, c, e : e + 1])
                h_tiles[e, c] = h_tile

        windows = []
        for a in range(m_blocks):
            window = psum.tile([P, S], F32, name=f"window_{a}")
            nc.tensor.matmul(window[:], ident[:], base_tiles[a // 2][:, a % 2, :], start=True, stop=False)
            windows.append(window)

        for a in range(m_blocks):
            for e in range(E):
                places = offsets[:, e * (Q // 16) : (e + 1) * (Q // 16)]
                for c in range(h_blocks):
                    nc.tensor.matmul(
                        windows[a][:].indirect(places),
                        w2_tiles[e][:, c, a * P : (a + 1) * P],
                        h_tiles[e, c][:],
                        start=False,
                        stop=e == E - 1 and c == h_blocks - 1,
                    )

        out_rows = out.rearrange("(a p) s -> a p s", p=P)
        for a in range(m_blocks):
            z = held.tile([P, S], F32, name=f"z_{a}")
            if a % 2 == 0:
                nc.vector.tensor_copy(z[:], windows[a][:])
            else:
                nc.scalar.copy(z[:], windows[a][:])
            nc.sync.dma_start(out_rows[a], z[:])
